import numpy as np
import ml_dtypes


def mxq(x, axis, fmt="e4m3"):
    dtype, down = {"e4m3": (ml_dtypes.float8_e4m3fn, 7), "e5m2": (ml_dtypes.float8_e5m2, 14)}[fmt]
    v = np.moveaxis(np.asarray(x, np.float32).astype(ml_dtypes.bfloat16).astype(np.float64), axis, -1)
    blocks = v.reshape(v.shape[:-1] + (-1, 32))
    amax = np.abs(blocks).max(-1, keepdims=True)
    byte = np.maximum(np.where(amax > 0, np.frexp(amax)[1] - 1 + 127, 0) - down, 1)
    scale = np.exp2(byte - 127.0)
    codes = (blocks / scale).astype(np.float32).astype(dtype).astype(np.float64)
    return np.moveaxis((codes * scale).reshape(v.shape), -1, axis)


WIDE = False


def mx_kscale(k):
    if not WIDE:
        return np.ones(k)
    levels = np.array([10, -10, 5, -5, 0])
    if k % 512:
        return np.exp2(np.random.permutation(np.resize(levels, k // 32))).repeat(32)
    a = np.empty((k // 512, 16))
    for p in range(k // 512):
        a[p, :8] = np.random.permutation(np.resize(levels, 8))
        for g in range(8):
            far = levels[np.abs(levels - a[p, g]) >= 10]
            a[p, g + 8] = far[np.random.randint(len(far))]
    return np.exp2(a.ravel()).repeat(32)


def f64(x):
    return np.asarray(x).astype(np.float64)


def striped(idx):
    return np.tile(idx.reshape(-1, 16).T, (8, 1)).astype(np.uint16)


def unstriped(offs):
    return offs[:16].T.reshape(-1).astype(np.int64)


def pack_weight(w):
    k, n = w.shape
    w = f64(np.asarray(w, np.float32).astype(ml_dtypes.bfloat16)).reshape(k // 32, 32, n)
    amax = np.abs(w).max(1)
    byte = np.clip(np.where(amax > 0, np.frexp(amax)[1] - 1 + 127 - 7, 1), 1, 254)
    scaled = (w * np.exp2(127.0 - byte)[:, None, :]).reshape(k, n).astype(np.float32)
    words = np.ascontiguousarray(scaled.reshape(k // 512, 128, 4, n).transpose(0, 1, 3, 2)).astype(ml_dtypes.float8_e4m3fn).view(np.uint8)
    return words, np.ascontiguousarray(byte.astype(np.uint8).reshape(k // 512, 16, n))


def unpack_weight(words, scales):
    g, p, n, _ = words.shape
    vals = np.ascontiguousarray(words).view(ml_dtypes.float8_e4m3fn).astype(np.float64) * np.repeat(np.exp2(scales.astype(np.float64) - 127.0), 8, axis=1)[..., None]
    return vals.transpose(0, 1, 3, 2).reshape(g * 512, n)


def silu(v):
    return v / (1.0 + np.exp(-np.maximum(v, -700.0)))


K, T, S, N = 1024, 1024, 512, 512


def setup_inputs():
    n = np.random.standard_normal
    s = mx_kscale(K)[:, None]
    words, scales = pack_weight(n((K, N)) / np.sqrt(K) / s)
    return {
        "xT": (n((K, S)) * s).astype(np.float32),
        "w_words": words,
        "w_scales": scales,
        "b": (0.3 * n((N, 1))).astype(np.float32),
        "gate": np.tile(np.random.uniform(0.2, 1.0, S), (N, 1)).astype(np.float32),
        "offs": striped(np.sort(np.random.permutation(T)[:S])),
    }


def reference(xT, w_words, w_scales, b, gate, offs):
    w = unpack_weight(w_words, w_scales)
    idx = unstriped(offs)
    xq = mxq(f64(xT), 0, "e4m3")
    y = w.T @ xq
    y = silu(y + f64(b))
    out = np.zeros((N, T))
    out[:, idx] = f64(gate) * y
    return out

@@ -1,0 +1,147 @@
+from contextlib import ExitStack
+
+import concourse.mybir as mybir
+from concourse.masks import make_identity
+
+K, T, S, N = 1024, 1024, 512, 512
+FLOPS = 2 * K * S * N
+
+F32 = mybir.dt.float32
+BF16 = mybir.dt.bfloat16
+I32 = mybir.dt.int32
+U32 = mybir.dt.uint32
+U16 = mybir.dt.uint16
+U8 = mybir.dt.uint8
+FP8X4 = mybir.dt.float8_e4m3fn_x4
+SILU = mybir.ActivationFunctionType.Silu
+MULT = mybir.AluOpType.mult
+
+P = 128
+PACK = 4
+PASSES = K // (P * PACK)
+BLOCKS = N // P
+SLICE = 128
+SLICES = S // SLICE
+STRIPE = 16
+
+
+def tile_picked_place_lin_silu_srt_l_kernel(tc, xT, w_words, w_scales, b, gate, offs, out):
+    nc = tc.nc
+    with ExitStack() as ctx:
+        keep = ctx.enter_context(tc.tile_pool(name="keep", bufs=1))
+        psum = ctx.enter_context(tc.psum_pool(name="psum", bufs=1))
+
+        offsets = keep.tile([P, S // STRIPE], U16, name="offsets")
+        w_codes = keep.tile([P, PASSES, N], U32, name="w_codes", align_bytes=64)
+        w_plane = keep.tile([P, PASSES, N], U8, name="w_plane", align_bytes=64)
+        x_codes = keep.tile([P, PASSES, S], U32, name="x_codes", align_bytes=64)
+        x_plane = keep.tile([P, PASSES, S], U8, name="x_plane", align_bytes=64)
+        gates = keep.tile([P, BLOCKS, S], F32, name="gates")
+        windows = [keep.tile([P, T], F32, name=f"window{c}") for c in range(BLOCKS)]
+        raw = {}
+        grouped = {}
+        for s in range(SLICES):
+            for a in range(PASSES):
+                raw[s, a] = keep.tile([P, PACK, SLICE], F32, name=f"raw{s}_{a}")
+                grouped[s, a] = keep.tile([P, SLICE * PACK], BF16, name=f"grouped{s}_{a}", align_bytes=64)
+        warm_in = keep.tile([P, 1], F32, name="warm_in")
+        warm_out = keep.tile([P, 1], F32, name="warm_out")
+        bias_rows = keep.tile([P, P], F32, name="bias_rows")
+        identity = keep.tile([P, P], F32, name="identity")
+        bias = keep.tile([P, BLOCKS], F32, name="bias")
+
+        x_view = xT.rearrange("(a p t) j -> a p t j", a=PASSES, t=PACK)
+        w_view = w_words.rearrange("a p n t -> p a (n t)").bitcast(I32)
+        gate_view = gate.rearrange("(c p) j -> p c j", p=P)
+
+        def load_x(s, a):
+            nc.sync.dma_start(out=raw[s, a][:], in_=x_view[a, :, :, s * SLICE : (s + 1) * SLICE])
+
+        def load_w(c0, c1):
+            nc.sync.dma_start(out=w_codes[:, :, c0 * P : c1 * P].bitcast(I32), in_=w_view[:, :, c0 * P : c1 * P])
+
+        def load_gate(c0, c1, j0, j1):
+            nc.sync.dma_start(out=gates[:, c0:c1, j0:j1], in_=gate_view[:, c0:c1, j0:j1])
+
+        def interleave(engine_copy, s, a):
+            engine_copy(
+                out=grouped[s, a][:].rearrange("p (c i t) -> p c t i", i=4, t=PACK),
+                in_=raw[s, a][:].rearrange("p t (c i) -> p c t i", i=4),
+            )
+
+        def quantize(s, a):
+            cols = slice(s * SLICE, (s + 1) * SLICE)
+            nc.vector.quantize_mx(out=x_codes[:, a, cols].bitcast(FP8X4), scales=x_plane[:, a, cols], in_=grouped[s, a][:])
+
+        def prepare(s):
+            interleave(nc.scalar.copy, s, 0)
+            interleave(nc.vector.tensor_copy, s, 1)
+            quantize(s, 0)
+            quantize(s, 1)
+
+        def place(c, j0, j1):
+            acc = psum.tile([P, j1 - j0], F32, name="acc", bufs=7)
+            for a in range(PASSES):
+                nc.tensor.matmul_mx(
+                    out=acc[:],
+                    lhsT=w_codes[:, a, c * P : (c + 1) * P].bitcast(FP8X4),
+                    lhsT_scale=w_plane[:, a, c * P : (c + 1) * P],
+                    rhs=x_codes[:, a, j0:j1].bitcast(FP8X4),
+                    rhs_scale=x_plane[:, a, j0:j1],
+                    start=(a == 0),
+                    stop=(a == PASSES - 1),
+                )
+            y = keep.tile([P, j1 - j0], F32, name=f"y{c}_{j0}")
+            nc.scalar.activation(out=y[:], in_=acc[:], func=SILU, bias=bias[:, c : c + 1])
+            nc.vector.tensor_tensor(
+                windows[c][:].indirect(offsets[:, j0 // STRIPE : j1 // STRIPE]), y[:], gates[:, c, j0:j1], MULT
+            )
+
+        def store(c):
+            nc.sync.dma_start(out=out[c * P : (c + 1) * P, :], in_=windows[c][:])
+
+        nc.vector.memset(w_plane[:].rearrange("p a n -> p (a n)").bitcast(I32), 0)
+        nc.gpsimd.memset(bias_rows[:], 0.0)
+        nc.gpsimd.dma_start(out=bias_rows[0:BLOCKS, :], in_=b.rearrange("(c p) o -> c (p o)", p=P))
+        make_identity(nc, identity[:])
+        nc.vector.memset(warm_in[:], 0.0)
+        nc.scalar.activation(out=warm_out[:], in_=warm_in[:], func=SILU)
+
+        load_x(0, 0)
+        load_x(0, 1)
+        load_w(0, 2)
+        scale_view = w_scales.bitcast(I32).rearrange("a (q r) n -> q r a n", r=4)
+        for q in range(4):
+            nc.sync.dma_start(out=w_plane[32 * q : 32 * q + 4, :, :].bitcast(I32), in_=scale_view[q])
+        load_x(1, 0)
+        load_gate(0, 2, 0, 128)
+        load_x(1, 1)
+        nc.sync.dma_start(offsets[:], offs)
+        load_gate(0, 2, 128, 384)
+        load_x(2, 0)
+        load_x(2, 1)
+        load_x(3, 0)
+        load_x(3, 1)
+        load_gate(0, 2, 384, 512)
+        load_w(2, 4)
+        load_gate(2, 3, 0, 512)
+        load_gate(3, 4, 0, 512)
+
+        for window in windows:
+            nc.vector.memset(window[:], 0.0)
+
+        bias_t = psum.tile([P, P], F32, name="bias_t")
+        nc.tensor.transpose(bias_t[:], bias_rows[:], identity[:])
+        nc.scalar.copy(out=bias[:], in_=bias_t[:, 0:BLOCKS])
+
+        for s in range(SLICES):
+            prepare(s)
+            place(0, s * SLICE, (s + 1) * SLICE)
+            if s == SLICES - 1:
+                store(0)
+            place(1, s * SLICE, (s + 1) * SLICE)
+        store(1)
+        for c in (2, 3):
+            place(c, 0, 256)
+            place(c, 256, 512)
+            store(c)

@@ -1,7 +1,6 @@
 from contextlib import ExitStack
 
 import concourse.mybir as mybir
-from concourse.masks import make_identity
 
 K, T, S, N = 1024, 1024, 512, 512
 FLOPS = 2 * K * S * N
@@ -20,9 +19,11 @@ P = 128
 PACK = 4
 PASSES = K // (P * PACK)
 BLOCKS = N // P
+HALF = S // 2
 SLICE = 128
-SLICES = S // SLICE
 STRIPE = 16
+QUADRANT = 32
+X_ROW = 12
 
 
 def tile_picked_place_lin_silu_srt_l_kernel(tc, xT, w_words, w_scales, b, gate, offs, out):
@@ -33,29 +34,25 @@ def tile_picked_place_lin_silu_srt_l_kernel(tc, xT, w_words, w_scales, b, gate, 
 
         offsets = keep.tile([P, S // STRIPE], U16, name="offsets")
         w_codes = keep.tile([P, PASSES, N], U32, name="w_codes", align_bytes=64)
-        w_plane = keep.tile([P, PASSES, N], U8, name="w_plane", align_bytes=64)
-        x_codes = keep.tile([P, PASSES, S], U32, name="x_codes", align_bytes=64)
-        x_plane = keep.tile([P, PASSES, S], U8, name="x_plane", align_bytes=64)
+        x_codes = keep.tile([P, 2, PASSES, HALF], U32, name="x_codes", align_bytes=64)
+        scales = keep.tile([P, 2 * PASSES * HALF], U8, name="scales", align_bytes=64)
         gates = keep.tile([P, BLOCKS, S], F32, name="gates")
         windows = [keep.tile([P, T], F32, name=f"window{c}") for c in range(BLOCKS)]
-        raw = {}
-        grouped = {}
-        for s in range(SLICES):
-            for a in range(PASSES):
-                raw[s, a] = keep.tile([P, PACK, SLICE], F32, name=f"raw{s}_{a}")
-                grouped[s, a] = keep.tile([P, SLICE * PACK], BF16, name=f"grouped{s}_{a}", align_bytes=64)
+        raw = keep.tile([P, 2, PASSES, PACK, HALF], F32, name="raw")
         warm_in = keep.tile([P, 1], F32, name="warm_in")
         warm_out = keep.tile([P, 1], F32, name="warm_out")
-        bias_rows = keep.tile([P, P], F32, name="bias_rows")
-        identity = keep.tile([P, P], F32, name="identity")
-        bias = keep.tile([P, BLOCKS], F32, name="bias")
+        bias_rows = keep.tile([P, P], F32, name="bias_rows", align_bytes=64)
+        bias = keep.tile([P, P], F32, name="bias", align_bytes=64)
+        banks = [psum.tile([P, HALF], F32, name=f"bank{i}") for i in range(4)]
 
         x_view = xT.rearrange("(a p t) j -> a p t j", a=PASSES, t=PACK)
         w_view = w_words.rearrange("a p n t -> p a (n t)").bitcast(I32)
+        scale_view = w_scales.bitcast(I32)
         gate_view = gate.rearrange("(c p) j -> p c j", p=P)
 
-        def load_x(s, a):
-            nc.sync.dma_start(out=raw[s, a][:], in_=x_view[a, :, :, s * SLICE : (s + 1) * SLICE])
+        def load_x(a, j0, j1):
+            h = j0 // HALF
+            nc.sync.dma_start(out=raw[:, h, a, :, j0 - h * HALF : j1 - h * HALF], in_=x_view[a, :, :, j0:j1])
 
         def load_w(c0, c1):
             nc.sync.dma_start(out=w_codes[:, :, c0 * P : c1 * P].bitcast(I32), in_=w_view[:, :, c0 * P : c1 * P])
@@ -63,85 +60,102 @@ def tile_picked_place_lin_silu_srt_l_kernel(tc, xT, w_words, w_scales, b, gate, 
         def load_gate(c0, c1, j0, j1):
             nc.sync.dma_start(out=gates[:, c0:c1, j0:j1], in_=gate_view[:, c0:c1, j0:j1])
 
-        def interleave(engine_copy, s, a):
+        def interleave(engine_copy, a, s, tag):
+            h, j0 = divmod(s * SLICE, HALF)
+            grouped = keep.tile([P, SLICE * PACK], BF16, name=f"grouped{a}_{s}", tag=tag, align_bytes=64)
             engine_copy(
-                out=grouped[s, a][:].rearrange("p (c i t) -> p c t i", i=4, t=PACK),
-                in_=raw[s, a][:].rearrange("p t (c i) -> p c t i", i=4),
+                out=grouped[:].rearrange("p (c i t) -> p c t i", i=4, t=PACK),
+                in_=raw[:, h, a, :, j0 : j0 + SLICE].rearrange("p t (c i) -> p c t i", i=4),
+            )
+            return grouped
+
+        def x_scale(h, a, j0, j1):
+            base = (h * PASSES + a) * HALF
+            return scales[X_ROW:P, base + j0 : base + j1]
+
+        def quantize(grouped, a, s):
+            h, j0 = divmod(s * SLICE, HALF)
+            nc.vector.quantize_mx(
+                out=x_codes[:, h, a, j0 : j0 + SLICE].bitcast(FP8X4), scales=x_scale(h, a, j0, j0 + SLICE), in_=grouped[:]
             )
 
-        def quantize(s, a):
-            cols = slice(s * SLICE, (s + 1) * SLICE)
-            nc.vector.quantize_mx(out=x_codes[:, a, cols].bitcast(FP8X4), scales=x_plane[:, a, cols], in_=grouped[s, a][:])
-
-        def prepare(s):
-            interleave(nc.scalar.copy, s, 0)
-            interleave(nc.vector.tensor_copy, s, 1)
-            quantize(s, 0)
-            quantize(s, 1)
-
-        def place(c, j0, j1):
-            acc = psum.tile([P, j1 - j0], F32, name="acc", bufs=7)
+        def product(c, h, bank, y):
             for a in range(PASSES):
                 nc.tensor.matmul_mx(
-                    out=acc[:],
+                    out=bank[:],
                     lhsT=w_codes[:, a, c * P : (c + 1) * P].bitcast(FP8X4),
-                    lhsT_scale=w_plane[:, a, c * P : (c + 1) * P],
-                    rhs=x_codes[:, a, j0:j1].bitcast(FP8X4),
-                    rhs_scale=x_plane[:, a, j0:j1],
+                    lhsT_scale=scales[4 * a : P, c * P : (c + 1) * P],
+                    rhs=x_codes[:, h, a, :].bitcast(FP8X4),
+                    rhs_scale=x_scale(h, a, 0, HALF),
                     start=(a == 0),
                     stop=(a == PASSES - 1),
                 )
-            y = keep.tile([P, j1 - j0], F32, name=f"y{c}_{j0}")
-            nc.scalar.activation(out=y[:], in_=acc[:], func=SILU, bias=bias[:, c : c + 1])
+            nc.scalar.activation(out=y, in_=bank[:], func=SILU, bias=bias[:, QUADRANT * c : QUADRANT * c + 1])
+
+        def scatter(c, j0, j1, y):
             nc.vector.tensor_tensor(
-                windows[c][:].indirect(offsets[:, j0 // STRIPE : j1 // STRIPE]), y[:], gates[:, c, j0:j1], MULT
+                windows[c][:].indirect(offsets[:, j0 // STRIPE : j1 // STRIPE]), y, gates[:, c, j0:j1], MULT
             )
 
         def store(c):
             nc.sync.dma_start(out=out[c * P : (c + 1) * P, :], in_=windows[c][:])
 
-        nc.vector.memset(w_plane[:].rearrange("p a n -> p (a n)").bitcast(I32), 0)
-        nc.gpsimd.memset(bias_rows[:], 0.0)
-        nc.gpsimd.dma_start(out=bias_rows[0:BLOCKS, :], in_=b.rearrange("(c p) o -> c (p o)", p=P))
-        make_identity(nc, identity[:])
         nc.vector.memset(warm_in[:], 0.0)
+        nc.vector.memset(bias_rows[:].bitcast(I32), 0)
         nc.scalar.activation(out=warm_out[:], in_=warm_in[:], func=SILU)
 
-        load_x(0, 0)
-        load_x(0, 1)
-        load_w(0, 2)
-        scale_view = w_scales.bitcast(I32).rearrange("a (q r) n -> q r a n", r=4)
+        load_x(0, 0, HALF)
         for q in range(4):
-            nc.sync.dma_start(out=w_plane[32 * q : 32 * q + 4, :, :].bitcast(I32), in_=scale_view[q])
-        load_x(1, 0)
-        load_gate(0, 2, 0, 128)
-        load_x(1, 1)
+            nc.sync.dma_start(
+                out=scales[QUADRANT * q : QUADRANT * q + 8, 0:N].bitcast(I32), in_=scale_view[:, 4 * q : 4 * q + 4, :]
+            )
+        load_x(1, 0, HALF)
+        nc.sync.dma_start(
+            out=bias_rows[0:P:QUADRANT, :].rearrange("q (c i) -> q c i", i=QUADRANT),
+            in_=b.rearrange("(c q i) o -> q c (i o)", q=4, i=QUADRANT),
+        )
+        load_x(0, HALF, S)
+        load_w(0, 2)
         nc.sync.dma_start(offsets[:], offs)
-        load_gate(0, 2, 128, 384)
-        load_x(2, 0)
-        load_x(2, 1)
-        load_x(3, 0)
-        load_x(3, 1)
-        load_gate(0, 2, 384, 512)
+        load_x(1, HALF, HALF + SLICE)
+        load_x(1, HALF + SLICE, S)
+        load_gate(0, 2, 0, HALF)
+        load_gate(0, 2, HALF, S)
         load_w(2, 4)
-        load_gate(2, 3, 0, 512)
-        load_gate(3, 4, 0, 512)
+        load_gate(2, 3, 0, S)
+        load_gate(3, 4, 0, S)
 
         for window in windows:
-            nc.vector.memset(window[:], 0.0)
+            nc.vector.memset(window[:].bitcast(I32), 0)
 
-        bias_t = psum.tile([P, P], F32, name="bias_t")
-        nc.tensor.transpose(bias_t[:], bias_rows[:], identity[:])
-        nc.scalar.copy(out=bias[:], in_=bias_t[:, 0:BLOCKS])
+        for a, s in ((0, 0), (1, 0), (0, 2)):
+            first = interleave(nc.vector.tensor_copy, a, s, f"stage{a}_{s}")
+            second = interleave(nc.scalar.copy, a, s + 1, f"stage{a}_{s + 1}")
+            quantize(first, a, s)
+            quantize(second, a, s + 1)
+        nc.vector.transpose(bias[:], bias_rows[:])
+        first = interleave(nc.scalar.copy, 1, 2, "stage1_2")
+        second = interleave(nc.vector.tensor_copy, 1, 3, "stage0_2")
+        quantize(first, 1, 2)
+        quantize(second, 1, 3)
 
-        for s in range(SLICES):
-            prepare(s)
-            place(0, s * SLICE, (s + 1) * SLICE)
-            if s == SLICES - 1:
-                store(0)
-            place(1, s * SLICE, (s + 1) * SLICE)
+        y00 = keep.tile([P, HALF], F32, name="y00", tag="stage0_3", align_bytes=64)
+        y10 = keep.tile([P, HALF], F32, name="y10")
+        y01 = keep.tile([P, HALF], F32, name="y01")
+        y11 = keep.tile([P, HALF], F32, name="y11")
+        product(0, 0, banks[0], y00[:])
+        product(1, 0, banks[1], y10[:])
+        product(0, 1, banks[2], y01[:])
+        product(1, 1, banks[3], y11[:])
+        scatter(0, 0, HALF, y00[:])
+        scatter(1, 0, HALF, y10[:])
+        scatter(0, HALF, S, y01[:])
+        store(0)
+        scatter(1, HALF, S, y11[:])
         store(1)
         for c in (2, 3):
-            place(c, 0, 256)
-            place(c, 256, 512)
+            y = keep.tile([P, S], F32, name=f"y{c}")
+            product(c, 0, banks[2], y[:, 0:HALF])
+            product(c, 1, banks[3], y[:, HALF:S])
+            scatter(c, 0, S, y[:])
             store(c)

@@ -33,39 +33,47 @@ def tile_picked_place_lin_silu_srt_l_kernel(tc, xT, w_words, w_scales, b, gate, 
         psum = ctx.enter_context(tc.psum_pool(name="psum", bufs=1))
 
         offsets = keep.tile([P, S // STRIPE], U16, name="offsets")
-        w_codes = keep.tile([P, PASSES, N], U32, name="w_codes", align_bytes=64)
         x_codes = keep.tile([P, 2, PASSES, HALF], U32, name="x_codes", align_bytes=64)
         scales = keep.tile([P, 2 * PASSES * HALF], U8, name="scales", align_bytes=64)
-        gates = keep.tile([P, BLOCKS, S], F32, name="gates")
         windows = [keep.tile([P, T], F32, name=f"window{c}") for c in range(BLOCKS)]
-        raw = keep.tile([P, 2, PASSES, PACK, HALF], F32, name="raw")
+        raw = {}
+        w_codes = {}
+        gates = {}
         warm_in = keep.tile([P, 1], F32, name="warm_in")
         warm_out = keep.tile([P, 1], F32, name="warm_out")
         bias_rows = keep.tile([P, P], F32, name="bias_rows", align_bytes=64)
         bias = keep.tile([P, P], F32, name="bias", align_bytes=64)
-        banks = [psum.tile([P, HALF], F32, name=f"bank{i}") for i in range(4)]
+        banks = [psum.tile([P, HALF], F32, name=f"bank{i}") for i in range(8)]
 
         x_view = xT.rearrange("(a p t) j -> a p t j", a=PASSES, t=PACK)
         w_view = w_words.rearrange("a p n t -> p a (n t)").bitcast(I32)
         scale_view = w_scales.bitcast(I32)
         gate_view = gate.rearrange("(c p) j -> p c j", p=P)
 
-        def load_x(a, j0, j1):
-            h = j0 // HALF
-            nc.sync.dma_start(out=raw[:, h, a, :, j0 - h * HALF : j1 - h * HALF], in_=x_view[a, :, :, j0:j1])
+        def load_x(a, s0, s1):
+            piece = keep.tile([P, PACK, (s1 - s0) * SLICE], F32, name=f"raw{a}_{s0}")
+            nc.sync.dma_start(out=piece[:], in_=x_view[a, :, :, s0 * SLICE : s1 * SLICE])
+            for s in range(s0, s1):
+                raw[a, s] = piece[:, :, (s - s0) * SLICE : (s - s0 + 1) * SLICE]
 
         def load_w(c0, c1):
-            nc.sync.dma_start(out=w_codes[:, :, c0 * P : c1 * P].bitcast(I32), in_=w_view[:, :, c0 * P : c1 * P])
+            piece = keep.tile([P, PASSES, (c1 - c0) * P], U32, name=f"w_codes{c0}", align_bytes=64)
+            nc.sync.dma_start(out=piece[:].bitcast(I32), in_=w_view[:, :, c0 * P : c1 * P])
+            for c in range(c0, c1):
+                for a in range(PASSES):
+                    w_codes[c, a] = piece[:, a, (c - c0) * P : (c - c0 + 1) * P]
 
         def load_gate(c0, c1, j0, j1):
-            nc.sync.dma_start(out=gates[:, c0:c1, j0:j1], in_=gate_view[:, c0:c1, j0:j1])
+            piece = keep.tile([P, c1 - c0, j1 - j0], F32, name=f"gate{c0}_{j0}")
+            nc.sync.dma_start(out=piece[:], in_=gate_view[:, c0:c1, j0:j1])
+            for c in range(c0, c1):
+                gates[c, j0] = piece[:, c - c0, :]
 
         def interleave(engine_copy, a, s, tag):
-            h, j0 = divmod(s * SLICE, HALF)
             grouped = keep.tile([P, SLICE * PACK], BF16, name=f"grouped{a}_{s}", tag=tag, align_bytes=64)
             engine_copy(
                 out=grouped[:].rearrange("p (c i t) -> p c t i", i=4, t=PACK),
-                in_=raw[:, h, a, :, j0 : j0 + SLICE].rearrange("p t (c i) -> p c t i", i=4),
+                in_=raw[a, s].rearrange("p t (c i) -> p c t i", i=4),
             )
             return grouped
 
@@ -83,7 +91,7 @@ def tile_picked_place_lin_silu_srt_l_kernel(tc, xT, w_words, w_scales, b, gate, 
             for a in range(PASSES):
                 nc.tensor.matmul_mx(
                     out=bank[:],
-                    lhsT=w_codes[:, a, c * P : (c + 1) * P].bitcast(FP8X4),
+                    lhsT=w_codes[c, a].bitcast(FP8X4),
                     lhsT_scale=scales[4 * a : P, c * P : (c + 1) * P],
                     rhs=x_codes[:, h, a, :].bitcast(FP8X4),
                     rhs_scale=x_scale(h, a, 0, HALF),
@@ -94,7 +102,7 @@ def tile_picked_place_lin_silu_srt_l_kernel(tc, xT, w_words, w_scales, b, gate, 
 
         def scatter(c, j0, j1, y):
             nc.vector.tensor_tensor(
-                windows[c][:].indirect(offsets[:, j0 // STRIPE : j1 // STRIPE]), y, gates[:, c, j0:j1], MULT
+                windows[c][:].indirect(offsets[:, j0 // STRIPE : j1 // STRIPE]), y, gates[c, j0], MULT
             )
 
         def store(c):
@@ -104,21 +112,22 @@ def tile_picked_place_lin_silu_srt_l_kernel(tc, xT, w_words, w_scales, b, gate, 
         nc.vector.memset(bias_rows[:].bitcast(I32), 0)
         nc.scalar.activation(out=warm_out[:], in_=warm_in[:], func=SILU)
 
-        load_x(0, 0, HALF)
+        load_x(0, 0, 2)
         for q in range(4):
             nc.sync.dma_start(
                 out=scales[QUADRANT * q : QUADRANT * q + 8, 0:N].bitcast(I32), in_=scale_view[:, 4 * q : 4 * q + 4, :]
             )
-        load_x(1, 0, HALF)
+        load_x(1, 0, 2)
+        load_x(0, 2, 4)
+        load_w(0, 1)
+        load_x(1, 2, 3)
         nc.sync.dma_start(
             out=bias_rows[0:P:QUADRANT, :].rearrange("q (c i) -> q c i", i=QUADRANT),
             in_=b.rearrange("(c q i) o -> q c (i o)", q=4, i=QUADRANT),
         )
-        load_x(0, HALF, S)
-        load_w(0, 2)
         nc.sync.dma_start(offsets[:], offs)
-        load_x(1, HALF, HALF + SLICE)
-        load_x(1, HALF + SLICE, S)
+        load_x(1, 3, 4)
+        load_w(1, 2)
         load_gate(0, 2, 0, HALF)
         load_gate(0, 2, HALF, S)
         load_w(2, 4)
@@ -139,7 +148,7 @@ def tile_picked_place_lin_silu_srt_l_kernel(tc, xT, w_words, w_scales, b, gate, 
         quantize(first, 1, 2)
         quantize(second, 1, 3)
 
-        y00 = keep.tile([P, HALF], F32, name="y00", tag="stage0_3", align_bytes=64)
+        y00 = keep.tile([P, HALF], F32, name="y00")
         y10 = keep.tile([P, HALF], F32, name="y10")
         y01 = keep.tile([P, HALF], F32, name="y01")
         y11 = keep.tile([P, HALF], F32, name="y11")
@@ -155,7 +164,7 @@ def tile_picked_place_lin_silu_srt_l_kernel(tc, xT, w_words, w_scales, b, gate, 
         store(1)
         for c in (2, 3):
             y = keep.tile([P, S], F32, name=f"y{c}")
-            product(c, 0, banks[2], y[:, 0:HALF])
-            product(c, 1, banks[3], y[:, HALF:S])
+            product(c, 0, banks[2 * c], y[:, 0:HALF])
+            product(c, 1, banks[2 * c + 1], y[:, HALF:S])
             scatter(c, 0, S, y[:])
             store(c)

@@ -19,11 +19,15 @@ P = 128
 PACK = 4
 PASSES = K // (P * PACK)
 BLOCKS = N // P
-HALF = S // 2
-SLICE = 128
+HALVES = 2
+HALF = S // HALVES
 STRIPE = 16
 QUADRANT = 32
-X_ROW = 12
+QUADRANTS = P // QUADRANT
+SCALE_ROWS = 4
+X_SCALE_ROW = 12
+LINE = 4
+VECTOR_SHARE = 160
 
 
 def tile_picked_place_lin_silu_srt_l_kernel(tc, xT, w_words, w_scales, b, gate, offs, out):
@@ -33,28 +37,35 @@ def tile_picked_place_lin_silu_srt_l_kernel(tc, xT, w_words, w_scales, b, gate, 
         psum = ctx.enter_context(tc.psum_pool(name="psum", bufs=1))
 
         offsets = keep.tile([P, S // STRIPE], U16, name="offsets")
-        x_codes = keep.tile([P, 2, PASSES, HALF], U32, name="x_codes", align_bytes=64)
-        scales = keep.tile([P, 2 * PASSES * HALF], U8, name="scales", align_bytes=64)
-        windows = [keep.tile([P, T], F32, name=f"window{c}") for c in range(BLOCKS)]
-        raw = {}
+        x_pass0 = keep.tile([P, PACK, S], F32, name="x_pass0")
+        x_pass1 = [keep.tile([P, PACK, HALF], F32, name=f"x_pass1_{h}") for h in range(HALVES)]
+        rounded_pass0 = [
+            keep.tile([P, HALF * PACK], BF16, name=f"rounded_pass0_{h}", align_bytes=64) for h in range(HALVES)
+        ]
+        rounded_pass1 = keep.tile([P, HALF * PACK], BF16, name="rounded_pass1", align_bytes=64)
+        rounded = {(h, a): rounded_pass1 if a else rounded_pass0[h] for h in range(HALVES) for a in range(PASSES)}
+        x_codes = keep.tile([P, HALVES, PASSES, HALF], U32, name="x_codes", align_bytes=64)
+        scales = keep.tile([P, HALVES * PASSES * HALF], U8, name="scales", align_bytes=64)
         w_codes = {}
-        gates = {}
-        warm_in = keep.tile([P, 1], F32, name="warm_in")
-        warm_out = keep.tile([P, 1], F32, name="warm_out")
+        gates = [keep.tile([P, S], F32, name=f"gate{c}") for c in range(BLOCKS)]
+        result_tiles = [keep.tile([P, S], F32, name=f"result{c}") for c in range(BLOCKS)]
+        results = {(c, h): result_tiles[c][:, h * HALF : (h + 1) * HALF] for c in range(BLOCKS) for h in range(HALVES)}
+        results[0, 0] = x_pass1[1][:, 0, :]
+        windows = [keep.tile([P, T], F32, name=f"window{c}") for c in range(BLOCKS)]
         bias_rows = keep.tile([P, P], F32, name="bias_rows", align_bytes=64)
         bias = keep.tile([P, P], F32, name="bias", align_bytes=64)
-        banks = [psum.tile([P, HALF], F32, name=f"bank{i}") for i in range(8)]
+        warm_in = keep.tile([P, 1], F32, name="warm_in")
+        warm_out = keep.tile([P, 1], F32, name="warm_out")
+        banks = {
+            (c, h): psum.tile([P, HALF], F32, name=f"bank{c}_{h}") for c in range(BLOCKS) for h in range(HALVES)
+        }
 
         x_view = xT.rearrange("(a p t) j -> a p t j", a=PASSES, t=PACK)
         w_view = w_words.rearrange("a p n t -> p a (n t)").bitcast(I32)
         scale_view = w_scales.bitcast(I32)
-        gate_view = gate.rearrange("(c p) j -> p c j", p=P)
 
-        def load_x(a, s0, s1):
-            piece = keep.tile([P, PACK, (s1 - s0) * SLICE], F32, name=f"raw{a}_{s0}")
-            nc.sync.dma_start(out=piece[:], in_=x_view[a, :, :, s0 * SLICE : s1 * SLICE])
-            for s in range(s0, s1):
-                raw[a, s] = piece[:, :, (s - s0) * SLICE : (s - s0 + 1) * SLICE]
+        def load_x_pass1(h):
+            nc.sync.dma_start(out=x_pass1[h][:], in_=x_view[1, :, :, h * HALF : (h + 1) * HALF])
 
         def load_w(c0, c1):
             piece = keep.tile([P, PASSES, (c1 - c0) * P], U32, name=f"w_codes{c0}", align_bytes=64)
@@ -63,108 +74,107 @@ def tile_picked_place_lin_silu_srt_l_kernel(tc, xT, w_words, w_scales, b, gate, 
                 for a in range(PASSES):
                     w_codes[c, a] = piece[:, a, (c - c0) * P : (c - c0 + 1) * P]
 
-        def load_gate(c0, c1, j0, j1):
-            piece = keep.tile([P, c1 - c0, j1 - j0], F32, name=f"gate{c0}_{j0}")
-            nc.sync.dma_start(out=piece[:], in_=gate_view[:, c0:c1, j0:j1])
-            for c in range(c0, c1):
-                gates[c, j0] = piece[:, c - c0, :]
+        def load_gate(c):
+            nc.sync.dma_start(out=gates[c][:], in_=gate[c * P : (c + 1) * P, :])
 
-        def interleave(engine_copy, a, s, tag):
-            grouped = keep.tile([P, SLICE * PACK], BF16, name=f"grouped{a}_{s}", tag=tag, align_bytes=64)
+        def round_x(engine_copy, h, a, j0, j1):
+            source = x_pass0[:, :, h * HALF + j0 : h * HALF + j1] if a == 0 else x_pass1[h][:, :, j0:j1]
             engine_copy(
-                out=grouped[:].rearrange("p (c i t) -> p c t i", i=4, t=PACK),
-                in_=raw[a, s].rearrange("p t (c i) -> p c t i", i=4),
-            )
-            return grouped
-
-        def x_scale(h, a, j0, j1):
-            base = (h * PASSES + a) * HALF
-            return scales[X_ROW:P, base + j0 : base + j1]
-
-        def quantize(grouped, a, s):
-            h, j0 = divmod(s * SLICE, HALF)
-            nc.vector.quantize_mx(
-                out=x_codes[:, h, a, j0 : j0 + SLICE].bitcast(FP8X4), scales=x_scale(h, a, j0, j0 + SLICE), in_=grouped[:]
+                out=rounded[h, a][:, j0 * PACK : j1 * PACK].rearrange("p (c i t) -> p c t i", i=LINE, t=PACK),
+                in_=source.rearrange("p t (c i) -> p c t i", i=LINE),
             )
 
-        def product(c, h, bank, y):
+        def round_x_shared(h, a):
+            round_x(nc.vector.tensor_copy, h, a, 0, VECTOR_SHARE)
+            round_x(nc.scalar.copy, h, a, VECTOR_SHARE, HALF)
+
+        def x_scale(h, a):
+            start = (h * PASSES + a) * HALF
+            return scales[X_SCALE_ROW:P, start : start + HALF]
+
+        def quantize(h, a):
+            nc.vector.quantize_mx(out=x_codes[:, h, a, :].bitcast(FP8X4), scales=x_scale(h, a), in_=rounded[h, a][:])
+
+        def product(c, h):
             for a in range(PASSES):
                 nc.tensor.matmul_mx(
-                    out=bank[:],
+                    out=banks[c, h][:],
                     lhsT=w_codes[c, a].bitcast(FP8X4),
-                    lhsT_scale=scales[4 * a : P, c * P : (c + 1) * P],
+                    lhsT_scale=scales[SCALE_ROWS * a : P, c * P : (c + 1) * P],
                     rhs=x_codes[:, h, a, :].bitcast(FP8X4),
-                    rhs_scale=x_scale(h, a, 0, HALF),
+                    rhs_scale=x_scale(h, a),
                     start=(a == 0),
                     stop=(a == PASSES - 1),
                 )
-            nc.scalar.activation(out=y, in_=bank[:], func=SILU, bias=bias[:, QUADRANT * c : QUADRANT * c + 1])
+            nc.scalar.activation(
+                out=results[c, h],
+                in_=banks[c, h][:],
+                func=SILU,
+                bias=bias[:, QUADRANT * c : QUADRANT * c + 1],
+            )
 
-        def scatter(c, j0, j1, y):
+        def scatter(c, j0, j1, values):
             nc.vector.tensor_tensor(
-                windows[c][:].indirect(offsets[:, j0 // STRIPE : j1 // STRIPE]), y, gates[c, j0], MULT
+                windows[c][:].indirect(offsets[:, j0 // STRIPE : j1 // STRIPE]),
+                values,
+                gates[c][:, j0:j1],
+                MULT,
             )
 
         def store(c):
             nc.sync.dma_start(out=out[c * P : (c + 1) * P, :], in_=windows[c][:])
 
-        nc.vector.memset(warm_in[:], 0.0)
         nc.vector.memset(bias_rows[:].bitcast(I32), 0)
+        nc.vector.memset(warm_in[:], 0.0)
         nc.scalar.activation(out=warm_out[:], in_=warm_in[:], func=SILU)
 
-        load_x(0, 0, 2)
-        for q in range(4):
+        nc.sync.dma_start(out=x_pass0[:, 0:2, :], in_=x_view[0, :, 0:2, :])
+        for q in range(QUADRANTS):
             nc.sync.dma_start(
-                out=scales[QUADRANT * q : QUADRANT * q + 8, 0:N].bitcast(I32), in_=scale_view[:, 4 * q : 4 * q + 4, :]
+                out=scales[QUADRANT * q : QUADRANT * q + PASSES * SCALE_ROWS, 0:N].bitcast(I32),
+                in_=scale_view[:, SCALE_ROWS * q : SCALE_ROWS * (q + 1), :],
             )
-        load_x(1, 0, 2)
-        load_x(0, 2, 4)
-        load_w(0, 1)
-        load_x(1, 2, 3)
+        nc.sync.dma_start(out=x_pass0[:, 2:4, :], in_=x_view[0, :, 2:4, :])
+        load_x_pass1(0)
         nc.sync.dma_start(
             out=bias_rows[0:P:QUADRANT, :].rearrange("q (c i) -> q c i", i=QUADRANT),
-            in_=b.rearrange("(c q i) o -> q c (i o)", q=4, i=QUADRANT),
+            in_=b.rearrange("(c q i) o -> q c (i o)", q=QUADRANTS, i=QUADRANT),
         )
+        load_w(0, 1)
         nc.sync.dma_start(offsets[:], offs)
-        load_x(1, 3, 4)
+        load_x_pass1(1)
         load_w(1, 2)
-        load_gate(0, 2, 0, HALF)
-        load_gate(0, 2, HALF, S)
-        load_w(2, 4)
-        load_gate(2, 3, 0, S)
-        load_gate(3, 4, 0, S)
+        load_gate(0)
+        load_gate(1)
+        load_w(2, BLOCKS)
+        load_gate(2)
+        load_gate(3)
 
         for window in windows:
             nc.vector.memset(window[:].bitcast(I32), 0)
 
-        for a, s in ((0, 0), (1, 0), (0, 2)):
-            first = interleave(nc.vector.tensor_copy, a, s, f"stage{a}_{s}")
-            second = interleave(nc.scalar.copy, a, s + 1, f"stage{a}_{s + 1}")
-            quantize(first, a, s)
-            quantize(second, a, s + 1)
+        vector_share_of_half1 = HALVES * VECTOR_SHARE - HALF
+        round_x(nc.vector.tensor_copy, 0, 0, 0, HALF)
+        round_x(nc.scalar.copy, 1, 0, vector_share_of_half1, HALF)
+        round_x(nc.vector.tensor_copy, 1, 0, 0, vector_share_of_half1)
+        quantize(0, 0)
+        round_x_shared(0, 1)
         nc.vector.transpose(bias[:], bias_rows[:])
-        first = interleave(nc.scalar.copy, 1, 2, "stage1_2")
-        second = interleave(nc.vector.tensor_copy, 1, 3, "stage0_2")
-        quantize(first, 1, 2)
-        quantize(second, 1, 3)
+        quantize(0, 1)
+        quantize(1, 0)
+        round_x_shared(1, 1)
+        quantize(1, 1)
 
-        y00 = keep.tile([P, HALF], F32, name="y00")
-        y10 = keep.tile([P, HALF], F32, name="y10")
-        y01 = keep.tile([P, HALF], F32, name="y01")
-        y11 = keep.tile([P, HALF], F32, name="y11")
-        product(0, 0, banks[0], y00[:])
-        product(1, 0, banks[1], y10[:])
-        product(0, 1, banks[2], y01[:])
-        product(1, 1, banks[3], y11[:])
-        scatter(0, 0, HALF, y00[:])
-        scatter(1, 0, HALF, y10[:])
-        scatter(0, HALF, S, y01[:])
-        store(0)
-        scatter(1, HALF, S, y11[:])
-        store(1)
+        for h in range(HALVES):
+            for c in (0, 1):
+                product(c, h)
+        for c in (0, 1):
+            scatter(c, 0, HALF, results[c, 0])
+        for c in (0, 1):
+            scatter(c, HALF, S, results[c, 1])
+            store(c)
         for c in (2, 3):
-            y = keep.tile([P, S], F32, name=f"y{c}")
-            product(c, 0, banks[2 * c], y[:, 0:HALF])
-            product(c, 1, banks[2 * c + 1], y[:, HALF:S])
-            scatter(c, 0, S, y[:])
+            for h in range(HALVES):
+                product(c, h)
+            scatter(c, 0, S, result_tiles[c][:])
             store(c)

from contextlib import ExitStack

import concourse.mybir as mybir

K, T, S, N = 1024, 1024, 512, 512
FLOPS = 2 * K * S * N

F32 = mybir.dt.float32
BF16 = mybir.dt.bfloat16
I32 = mybir.dt.int32
U32 = mybir.dt.uint32
U16 = mybir.dt.uint16
U8 = mybir.dt.uint8
FP8X4 = mybir.dt.float8_e4m3fn_x4
SILU = mybir.ActivationFunctionType.Silu
MULT = mybir.AluOpType.mult

P = 128
PACK = 4
PASSES = K // (P * PACK)
BLOCKS = N // P
HALVES = 2
HALF = S // HALVES
STRIPE = 16
QUADRANT = 32
QUADRANTS = P // QUADRANT
SCALE_ROWS = 4
X_SCALE_ROW = 12
LINE = 4
VECTOR_SHARE = 160


def tile_picked_place_lin_silu_srt_l_kernel(tc, xT, w_words, w_scales, b, gate, offs, out):
    nc = tc.nc
    with ExitStack() as ctx:
        keep = ctx.enter_context(tc.tile_pool(name="keep", bufs=1))
        psum = ctx.enter_context(tc.psum_pool(name="psum", bufs=1))

        offsets = keep.tile([P, S // STRIPE], U16, name="offsets")
        x_pass0 = keep.tile([P, PACK, S], F32, name="x_pass0")
        x_pass1 = [keep.tile([P, PACK, HALF], F32, name=f"x_pass1_{h}") for h in range(HALVES)]
        rounded_pass0 = [
            keep.tile([P, HALF * PACK], BF16, name=f"rounded_pass0_{h}", align_bytes=64) for h in range(HALVES)
        ]
        rounded_pass1 = keep.tile([P, HALF * PACK], BF16, name="rounded_pass1", align_bytes=64)
        rounded = {(h, a): rounded_pass1 if a else rounded_pass0[h] for h in range(HALVES) for a in range(PASSES)}
        x_codes = keep.tile([P, HALVES, PASSES, HALF], U32, name="x_codes", align_bytes=64)
        scales = keep.tile([P, HALVES * PASSES * HALF], U8, name="scales", align_bytes=64)
        w_codes = {}
        gates = [keep.tile([P, S], F32, name=f"gate{c}") for c in range(BLOCKS)]
        result_tiles = [keep.tile([P, S], F32, name=f"result{c}") for c in range(BLOCKS)]
        results = {(c, h): result_tiles[c][:, h * HALF : (h + 1) * HALF] for c in range(BLOCKS) for h in range(HALVES)}
        results[0, 0] = x_pass1[1][:, 0, :]
        windows = [keep.tile([P, T], F32, name=f"window{c}") for c in range(BLOCKS)]
        bias_rows = keep.tile([P, P], F32, name="bias_rows", align_bytes=64)
        bias = keep.tile([P, P], F32, name="bias", align_bytes=64)
        warm_in = keep.tile([P, 1], F32, name="warm_in")
        warm_out = keep.tile([P, 1], F32, name="warm_out")
        banks = {
            (c, h): psum.tile([P, HALF], F32, name=f"bank{c}_{h}") for c in range(BLOCKS) for h in range(HALVES)
        }

        x_view = xT.rearrange("(a p t) j -> a p t j", a=PASSES, t=PACK)
        w_view = w_words.rearrange("a p n t -> p a (n t)").bitcast(I32)
        scale_view = w_scales.bitcast(I32)

        def load_x_pass1(h):
            nc.sync.dma_start(out=x_pass1[h][:], in_=x_view[1, :, :, h * HALF : (h + 1) * HALF])

        def load_w(c0, c1):
            piece = keep.tile([P, PASSES, (c1 - c0) * P], U32, name=f"w_codes{c0}", align_bytes=64)
            nc.sync.dma_start(out=piece[:].bitcast(I32), in_=w_view[:, :, c0 * P : c1 * P])
            for c in range(c0, c1):
                for a in range(PASSES):
                    w_codes[c, a] = piece[:, a, (c - c0) * P : (c - c0 + 1) * P]

        def load_gate(c):
            nc.sync.dma_start(out=gates[c][:], in_=gate[c * P : (c + 1) * P, :])

        def round_x(engine_copy, h, a, j0, j1):
            source = x_pass0[:, :, h * HALF + j0 : h * HALF + j1] if a == 0 else x_pass1[h][:, :, j0:j1]
            engine_copy(
                out=rounded[h, a][:, j0 * PACK : j1 * PACK].rearrange("p (c i t) -> p c t i", i=LINE, t=PACK),
                in_=source.rearrange("p t (c i) -> p c t i", i=LINE),
            )

        def round_x_shared(h, a):
            round_x(nc.vector.tensor_copy, h, a, 0, VECTOR_SHARE)
            round_x(nc.scalar.copy, h, a, VECTOR_SHARE, HALF)

        def x_scale(h, a):
            start = (h * PASSES + a) * HALF
            return scales[X_SCALE_ROW:P, start : start + HALF]

        def quantize(h, a):
            nc.vector.quantize_mx(out=x_codes[:, h, a, :].bitcast(FP8X4), scales=x_scale(h, a), in_=rounded[h, a][:])

        def product(c, h):
            for a in range(PASSES):
                nc.tensor.matmul_mx(
                    out=banks[c, h][:],
                    lhsT=w_codes[c, a].bitcast(FP8X4),
                    lhsT_scale=scales[SCALE_ROWS * a : P, c * P : (c + 1) * P],
                    rhs=x_codes[:, h, a, :].bitcast(FP8X4),
                    rhs_scale=x_scale(h, a),
                    start=(a == 0),
                    stop=(a == PASSES - 1),
                )
            nc.scalar.activation(
                out=results[c, h],
                in_=banks[c, h][:],
                func=SILU,
                bias=bias[:, QUADRANT * c : QUADRANT * c + 1],
            )

        def scatter(c, j0, j1, values):
            nc.vector.tensor_tensor(
                windows[c][:].indirect(offsets[:, j0 // STRIPE : j1 // STRIPE]),
                values,
                gates[c][:, j0:j1],
                MULT,
            )

        def store(c):
            nc.sync.dma_start(out=out[c * P : (c + 1) * P, :], in_=windows[c][:])

        nc.vector.memset(bias_rows[:].bitcast(I32), 0)
        nc.vector.memset(warm_in[:], 0.0)
        nc.scalar.activation(out=warm_out[:], in_=warm_in[:], func=SILU)

        nc.sync.dma_start(out=x_pass0[:, 0:2, :], in_=x_view[0, :, 0:2, :])
        for q in range(QUADRANTS):
            nc.sync.dma_start(
                out=scales[QUADRANT * q : QUADRANT * q + PASSES * SCALE_ROWS, 0:N].bitcast(I32),
                in_=scale_view[:, SCALE_ROWS * q : SCALE_ROWS * (q + 1), :],
            )
        nc.sync.dma_start(out=x_pass0[:, 2:4, :], in_=x_view[0, :, 2:4, :])
        load_x_pass1(0)
        nc.sync.dma_start(
            out=bias_rows[0:P:QUADRANT, :].rearrange("q (c i) -> q c i", i=QUADRANT),
            in_=b.rearrange("(c q i) o -> q c (i o)", q=QUADRANTS, i=QUADRANT),
        )
        load_w(0, 1)
        nc.sync.dma_start(offsets[:], offs)
        load_x_pass1(1)
        load_w(1, 2)
        load_gate(0)
        load_gate(1)
        load_w(2, BLOCKS)
        load_gate(2)
        load_gate(3)

        for window in windows:
            nc.vector.memset(window[:].bitcast(I32), 0)

        vector_share_of_half1 = HALVES * VECTOR_SHARE - HALF
        round_x(nc.vector.tensor_copy, 0, 0, 0, HALF)
        round_x(nc.scalar.copy, 1, 0, vector_share_of_half1, HALF)
        round_x(nc.vector.tensor_copy, 1, 0, 0, vector_share_of_half1)
        quantize(0, 0)
        round_x_shared(0, 1)
        nc.vector.transpose(bias[:], bias_rows[:])
        quantize(0, 1)
        quantize(1, 0)
        round_x_shared(1, 1)
        quantize(1, 1)

        for h in range(HALVES):
            for c in (0, 1):
                product(c, h)
        for c in (0, 1):
            scatter(c, 0, HALF, results[c, 0])
        for c in (0, 1):
            scatter(c, HALF, S, results[c, 1])
            store(c)
        for c in (2, 3):
            for h in range(HALVES):
                product(c, h)
            scatter(c, 0, S, result_tiles[c][:])
            store(c)
